import numpy as np, ml_dtypes
CORES = [16,17,18,19,32,33,34,35]
N = 8
BF = ml_dtypes.bfloat16
def gentries(a):
    return np.ascontiguousarray(a.reshape(8, 16, -1).transpose(0, 2, 1)).reshape(8, -1)
def gtable(e):
    e = np.asarray(e); return np.ascontiguousarray(e.reshape(8, -1, 16).transpose(0, 2, 1)).reshape(128, -1).astype(np.int32)
W, NB, P, Q, RO, ST, LO, HI, OWN = 8192, 1024, 512, 16, 3, 3, 5, 8, 1
def sites(rng):
    b = np.argsort(rng.random((N, 8, NB)), axis=-1); o = np.argsort(rng.random((N, 8, NB)), axis=-1)
    return b, np.ascontiguousarray(o[..., :P]), np.take_along_axis(b, o[..., P:], -1)
def some(rng):
    x = rng.integers(0, 256, (N, 8, 16, W), dtype=np.int16); c = rng.integers(0, W, (N, 8, 16, NB))
    pf = rng.integers(0, 256, (N, 8, 16, P)); pn = rng.integers(0, 256, (N, 8, 16, P))
    th = (rng.choice(np.array([1, 60, 400]), (N, 8, 1)) * rng.random((N, 8, 16))).astype(np.int64)
    return x, c, pf, pn, th
def lay(b, fl, nu, ca, ch):
    c = np.zeros((N, 8, 16, NB), np.int64); a = np.take_along_axis(b, fl, -1)
    np.put_along_axis(c, a[:, :, None, :], ca, 3); np.put_along_axis(c, nu[:, :, None, :], ch, 3)
    return c
def pack(x, c, b, fl, nu, pf, pn, th):
    return {"xf": x.reshape(N, 128, W).astype(np.float32).astype(BF), "cb": np.ascontiguousarray(c.reshape(N, 128, NB)).astype(np.int32), "bs": np.stack([gtable(v) for v in b]),
            "fs": np.stack([gtable(v) for v in fl]), "nb": np.stack([gtable(v) for v in nu]), "pf": pf.reshape(N, 128, P).astype(np.float32).astype(BF),
            "pn": pn.reshape(N, 128, P).astype(np.float32).astype(BF), "th": np.ascontiguousarray(th.reshape(N, 128, 1)).astype(np.int32)}
def setup_inputs(rng):
    b, fl, nu = sites(rng); x, c, pf, pn, th = some(rng)
    return pack(x, c, b, fl, nu, pf, pn, th)
def setup_inputs_corners(rng):
    b, fl, nu = sites(rng)
    for q in range(N):
        for g in range(8):
            if g in (0, 3): b[q, g] = np.arange(NB)
            if g == 1: b[q, g] = np.arange(NB)[::-1]
            o = np.concatenate([fl[q, g], np.setdiff1d(np.arange(NB), fl[q, g])])
            if g == 2: o = np.concatenate([np.arange(0, NB, 2), rng.permutation(np.arange(1, NB, 2))])
            if g == 3: o = np.arange(NB)
            if g == 4: o = np.arange(NB)[::-1]
            if g == 5: o = np.concatenate([rng.permutation(P), P + rng.permutation(P)])
            fl[q, g] = o[:P]; nu[q, g] = b[q, g][o[P:]]
    order = np.argsort(rng.random((N, 8, W)), axis=-1)
    order[:, 6:] = order[0, 6:].copy()
    tot = np.concatenate([np.broadcast_to(np.arange(4081), (N, 8, 4081)), rng.integers(0, 4081, (N, 8, W - 4081))], axis=2)
    sg = np.zeros((N, 8, W), np.int64); np.put_along_axis(sg, order, tot, 2); sg = sg[:, :, None, :]
    ln = (np.arange(16)[:, None] + np.arange(W)[None, :]) % 16
    x = (sg // 16 + (ln[None, None] < sg % 16)).astype(np.int16); loc = order[:, :, None, :4081]
    th = rng.choice(np.array([0, 1, 2, 7, 300, 1001, 4095, 4096, 6001, 8158, 8159]), (N, 8, 16)); th[:, 6:] = rng.integers(1002, 4160, (N, 2, 16))
    want = rng.choice(np.array([0, LO, LO + 1, HI - 1, HI, 16]), (N, 8, P))
    for q in range(N):
        for g in range(8):
            m = (g + q) % 8
            if m < 4: want[q, g] = rng.choice(np.array(((HI, 16), (0, LO), (LO + 1, HI - 1), (16, 16))[m]), P)
    sw = np.argsort(np.argsort(rng.random((N, 8, 16, P)), axis=2), axis=2) < want[:, :, None, :]
    d = th[..., None] // 2 + sw; lo = (rng.random((N, 8, 16, P)) * (4081 - d)).astype(np.int64)
    ch = np.take_along_axis(loc, lo + d, 3); cl = np.take_along_axis(loc, lo, 3)
    u = rng.integers(0, 2, (N, 8, 1, P)); z = np.zeros((N, 8, 16, P), np.int64)
    ca = np.where(u == 0, ch, cl); cc = np.where(u == 0, cl, ch)
    mv = rng.random(P) < 0.5; mv[0] = True; mv[P - 1] = False
    u[:, 6, 0] = np.where(mv, rng.integers(0, 2, P), np.arange(N)[:, None] % 2); u[:, 7] = rng.integers(0, 2)
    for g in (6, 7):
        small, large = [w[(w & (min(Q, 16) - 1)) > 0] for w in (order[0, g, :1001], order[0, g, 3080:4081])]
        small = rng.choice(small, (N, 16, P)); large = rng.choice(large, (N, 16, P)); up = u[:, g] == 0
        if g == 6: up = up != mv
        ca[:, g] = np.where(up, large, small); cc[:, g] = np.where(up, small, large)
    return pack(x, lay(b, fl, nu, ca, cc), b, fl, nu, z + 255 * u, z + 255 * (1 - u), th)
def setup_inputs_ends(rng):
    o = 1 + np.argsort(rng.random((N, 8, NB - 2)), axis=-1); k = 1 + np.argsort(rng.random((N, 8, NB - 2)), axis=-1)
    z = np.zeros((N, 8, 1), np.int64); fl = np.concatenate([z, o[..., :P - 2], z + NB - 1], axis=2); nu = np.concatenate([z, k[..., :P - 2], z + NB - 1], axis=2)
    b = np.zeros((N, 8, NB), np.int64); np.put_along_axis(b, fl, k[..., P - 2:], 2); np.put_along_axis(b, o[..., P - 2:], nu, 2)
    rk = 1 + np.argsort(rng.random((N, 8, W - 2)), axis=-1); n = 2 * W // 5; low = rk[:, :, None, :n]; high = rk[:, :, None, n:2 * n]
    x = rng.integers(0, 2, (N, 8, 16, W), dtype=np.int16) * np.int16(255)
    np.put_along_axis(x, low, 0, 3); np.put_along_axis(x, high, 255, 3)
    e = rng.integers(0, 2, (N, 8)); e[N - 1, 7] = 0
    x[..., 0] = 255 * e[:, :, None]; x[..., W - 1] = 255 * (1 - e)[:, :, None]
    eh = np.where(e == 1, 0, W - 1)[:, :, None, None]; el = W - 1 - eh; sh = (N, 8, 16, P)
    ch = np.where(rng.random(sh) < 0.75, eh, np.take_along_axis(high, rng.integers(0, n, sh), 3))
    cl = np.where(rng.random(sh) < 0.75, el, np.take_along_axis(low, rng.integers(0, n, sh), 3))
    u = rng.choice(np.array([0, 0, 1, 1, 2]), (N, 8, 1, P)); u[0] = rng.integers(0, 2, (8, 1, P)); u[N - 1] = rng.integers(0, 2, (8, 1, P)); u[N - 1, 7, 0, P - 1] = 0
    pf = np.where(u == 0, 0, np.where(u == 1, 255, 255 * rng.integers(0, 2, sh))); pn = np.where(u == 0, 255, np.where(u == 1, 0, 255 * rng.integers(0, 2, sh)))
    th = 8159 * rng.integers(0, 2, (N, 8, 16)); th[:, 0, 0] = 0; th[:, 7, 15] = 8159
    w = rng.choice(np.array([0.0, 0.3, 0.6, 0.8, 1.0]), (N, 8, 1, P)); w[0] = 0.0; w[N - 1] = 1.0
    up = (rng.random(sh) < w) == (u == 0); ca = np.where(up, ch, cl); cc = np.where(up, cl, ch)
    tie = rng.random(sh) < 0.1; tie[0] = False; tie[N - 1] = False
    return pack(x, lay(b, fl, nu, ca, np.where(tie, ca, cc)), b, fl, nu, pf, pn, th)
def setup_inputs_fresh(rng):
    b, fl, nu = sites(rng); x, c, pf, pn, th = some(rng); sh = (N, 8, 16, NB)
    sm = np.add.reduce(pf, axis=2); i = rng.integers(0, P, sh); r = np.arange(N)[:, None, None, None]; g = np.arange(8)[None, :, None, None]
    q = (r + ST * rng.integers(0, RO, sh)) % N
    c = np.where(rng.random(sh) < 0.9, Q * i + ((sm[q, g, i] + rng.integers(3, 11, sh)) & (Q - 1)), c)
    return pack(x, c, b, fl, nu, pf, pn, th)
def setup_inputs_spread(rng):
    b, fl, nu = sites(rng)
    x = np.minimum(np.exp2(8.01 * rng.random((N, 8, 1, W), dtype=np.float32)) * rng.random((N, 8, 16, W), dtype=np.float32), 255).astype(np.int16)
    pf = np.minimum(np.exp2(2 + 6.01 * rng.random((N, 8, 1, P))) * rng.random((N, 8, 16, P)), 255).astype(np.int64)
    pn = np.minimum(np.exp2(2 + 6.01 * rng.random((N, 8, 1, P))) * rng.random((N, 8, 16, P)), 255).astype(np.int64)
    c = np.minimum((W * rng.random((N, 8, 16, NB)) ** 3).astype(np.int64), W - 1); c = np.where(rng.random((N, 8, 1, NB)) < 0.5, c, W - 1 - c)
    kind = rng.choice(np.array([0.25, 0.25, 0.5, 1.0]), (N, 8, 1))
    th = np.minimum(np.exp2(13 * kind * rng.random((N, 8, 16))).astype(np.int64) - 1, 8159)
    return pack(x, c, b, fl, nu, pf, pn, th)
def check_inputs(d):
    bad = []
    for k, lo, hi in (("xf", 0, 255), ("cb", 0, W - 1), ("bs", 0, NB - 1), ("fs", 0, NB - 1), ("nb", 0, NB - 1), ("pf", 0, 255), ("pn", 0, 255), ("th", 0, 8159)):
        v = np.asarray(d[k]).astype(np.float32)
        if not (np.all(v >= lo) and np.all(v <= hi)): bad.append("range of " + k)
        elif np.any(v != np.floor(v)): bad.append("whole numbers of " + k)
    b, fl, nu = [np.stack([gentries(np.clip(np.asarray(v), 0, NB - 1).astype(np.int64)) for v in d[k]]) for k in ("bs", "fs", "nb")]
    if np.any(np.sort(b, axis=-1) != np.arange(NB)): bad.append("bs: a permutation of the boxes in every group")
    if np.any(np.sort(np.concatenate([np.take_along_axis(b, fl, -1), nu], axis=2), axis=-1) != np.arange(NB)): bad.append("fs, nb: the flyers' boxes and the nurses' boxes are all boxes, each once")
    return bad
def reference(xf, cb, bs, fs, nb, pf, pn, th):
    x = xf.astype(np.float32).astype(np.int32).reshape(N, 8, 16, W); c = cb.astype(np.int64).reshape(N, 8, 16, NB)
    b, fl, nu = [np.stack([gentries(v) for v in k]).astype(np.int64) for k in (bs, fs, nb)]
    rf = pf.astype(np.float32).astype(np.int32).reshape(N, 8, 16, P); rn = pn.astype(np.float32).astype(np.int32).reshape(N, 8, 16, P); lim = th.astype(np.int64).reshape(N, 8, 16, 1)
    for t in range(RO):
        for r in range(N):
            q = (r + ST * t) % N
            box = np.take_along_axis(b[r], fl[r], 1); nur = nu[r].copy()
            ca = np.take_along_axis(c[r], box[:, None, :], 2); ch = np.take_along_axis(c[r], nur[:, None, :], 2)
            xa = np.take_along_axis(x[q], ca.reshape(8, 1, 16 * P), 2).reshape(8, 16, 16, P)
            xh = np.take_along_axis(x[q], ch.reshape(8, 1, 16 * P), 2).reshape(8, 16, 16, P)
            u = rf[q][:, :, None, :]; v = rn[q][:, :, None, :]
            score = np.add.reduce(np.abs(xa - u) + np.abs(xh - v) - np.abs(xh - u) - np.abs(xa - v), axis=1)
            sw = score > lim[q]; s = np.add.reduce(sw.astype(np.int64), axis=1)
            np.put_along_axis(c[r], box[:, None, :], np.where(sw, ch, ca), 2); np.put_along_axis(c[r], nur[:, None, :], np.where(sw, ca, ch), 2)
            flag = np.zeros((8, NB), bool); np.put_along_axis(flag, fl[r], s >= HI, 1)
            inv = np.argsort(b[r], axis=1); turn = s <= LO
            fl[r] = np.where(turn, np.take_along_axis(inv, nur, 1), fl[r]); nu[r] = np.where(turn, box, nur)
            total = np.add.reduce(s, axis=1)[:, None]
            if not OWN: total = np.zeros((8, 1), np.int64) + np.add.reduce(total, axis=None)
            mate = np.arange(NB)[None, :] ^ ((total & (NB - 1)) | 1)
            both = flag & np.take_along_axis(flag, mate, 1)
            b[r] = np.where(both, np.take_along_axis(b[r], mate, 1), b[r])
            col = Q * np.arange(P)[None, :] + ((np.add.reduce(rf[q].astype(np.int64), axis=1) + s) & (Q - 1))
            np.put_along_axis(x[q], col[:, None, :], rf[q], 2)
    who = [(q - ST * (RO - 1)) % N for q in range(N)]
    return {"yc": c[who].reshape(N, 128, NB).astype(np.float32), "yb": np.stack([gtable(b[r]) for r in who]).astype(np.float32),
            "yf": np.stack([gtable(fl[r]) for r in who]).astype(np.float32), "yn": np.stack([gtable(nu[r]) for r in who]).astype(np.float32)}

import math
from concourse.mybir import dt, AluOpType, AxisListType, ActivationFunctionType

OP = AluOpType
AF = ActivationFunctionType
NCH = 8
LOOK = 3
NZ = 4
EL = 2048

SB = {
    "Xw": (8192, "bfloat16"), "D0": (8 * EL, "bfloat16"), "D1": (8 * EL, "bfloat16"),
    "pfb": (512, "bfloat16"), "pnb": (512, "bfloat16"), "sg": (512, "bfloat16"), "c1": (512, "bfloat16"),
    "c2": (512, "bfloat16"), "swp": (512, "bfloat16"), "swR": (1024, "bfloat16"),
    "SEp": (4096, "bfloat16"), "SEn": (4096, "bfloat16"), "FJ": (4096, "bfloat16"), "BJ": (64, "bfloat16"),
    "LJ": (4096, "bfloat16"), "QJ": (4, "bfloat16"), "qji": (4, "float32"),
    "TM": (128, "float32"), "THh": (128, "bfloat16"), "THl": (128, "bfloat16"), "GE": (256, "bfloat16"), "gi": (256, "float32"),
    "thi": (1, "int32"), "cI": (8, "int32"), "cF": (16, "float32"),
    "cbi": (1024, "int32"), "bsi": (64, "int32"), "fsi": (32, "int32"), "nbi": (32, "int32"),
    "bu": (64, "uint16"), "nu": (32, "uint16"),
    "iot": (1024, "float32"), "iotk": (1024, "float32"), "bigA": (1024, "float32"), "bigB": (1024, "float32"),
    "tab": (1024, "float32"), "jb": (512, "float32"), "M16": (512, "float32"), "R16": (512, "float32"),
    "slot1": (512, "float32"), "val": (512, "float32"), "tmp": (512, "float32"), "tmp2": (512, "float32"),
    "A2f": (512, "float32"), "dHA": (512, "float32"), "sgf": (512, "float32"),
    "W": (2048, "bfloat16"), "Dri": (2048, "float32"), "mdiv": (128, "float32"),
    "BOb": (128, "bfloat16"), "Ib": (128, "bfloat16"), "BOf": (128, "float32"),
    "E8": (8, "float32"), "E8n": (8, "float32"),
    "bji": (64, "float32"), "slotl": (32, "float32"), "own1": (32, "float32"), "n256": (32, "int32"), "baseI": (32, "int32"),
    "eI": (32, "int32"), "eJ": (32, "int32"), "eL2": (32, "float32"),
    "hu": (512, "uint16"), "ao": (512, "uint16"), "pu": (32, "uint16"), "Fi": (32, "int32"), "VB": (320, "int32"),
    "U": (320, "float32"), "F0": (32, "float32"), "DQP": (64, "float32"), "XB": (320, "bfloat16"),
    "Xl": (32, "float32"), "Xu": (32, "uint16"), "o1": (32, "int32"), "o2": (32, "int32"), "o3": (32, "int32"), "offU": (32, "uint16"),
    "r10": (16, "float32"), "p2i": (16, "float32"), "pwI": (16, "int32"), "yI": (16, "int32"), "bI": (16, "int32"),
    "E10": (16, "float32"), "T2": (64, "float32"), "td": (64, "float32"), "fl": (32, "float32"), "b1": (32, "float32"),
    "BB": (64, "float32"), "qi": (32, "int32"), "dec": (64, "int32"), "df": (64, "float32"), "df2": (64, "float32"),
    "asf": (32, "float32"), "asu": (32, "uint16"), "cu": (32, "uint16"), "gu": (32, "uint16"), "fu": (32, "uint16"), "au": (32, "uint16"),
    "ybo": (64, "float32"),
}
COL = {k: ("cI", x) for x, k in enumerate(["pI", "pmI", "pqI", "th2", "thA", "thB", "phI"])}
COL.update({k: ("cF", x) for x, k in enumerate(["colp", "colm", "colq", "colm16", "cold", "thC", "thD", "red", "colh"])})
for _z in range(NZ):
    SB["Z%d" % _z] = (EL, "bfloat16")
for _t in range(3):
    SB["AHi%d" % _t] = (1024, "float32")
    SB["AHo%d" % _t] = (1024, "float32")
    SB["LSi%d" % _t] = (160, "float32")
    SB["LSo%d" % _t] = (160, "float32")
PS = ["psR0", "psR1", "psR2", "psR3", "psC0", "psC1", "psL", "psM"]
SCRATCH = {k: ("sbuf", [128, v[0]], v[1]) for k, v in SB.items()}
for _p in PS:
    SCRATCH[_p] = ("psum", [128, 512], "float32")
LOADS = ["fs", "nb", "bs", "cb", "pf", "pn", "th", "x0", "x1", "x2", "x3"]
STORES = ["yc", "yb", "yf", "yn"]
SEMAPHORES = (["qv", "qs", "qp", "qg", "sent"] + ["ld_" + k for k in LOADS] + ["st_" + k for k in STORES]
              + ["ah%d_%d" % (t, m) for t in (1, 2) for m in range(4)] + ["ls1", "ls2"])


def meets(a, b):
    if a[1] >= b[2] or b[1] >= a[2]:
        return False
    d = math.gcd(a[3], b[3])
    return not (d > 1 and (a[1] - b[1]) % d)


def inside(e, w):
    return e[1] >= w[1] and e[2] <= w[2] and (w[3] == 1 or (e[3] % w[3] == 0 and (e[1] - w[1]) % w[3] == 0))


def rank_program(g, core, T, topo):
    rank = T.rank_of(core)
    if rank is None:
        return
    n = len(T.cores)
    nxt, prv = T.cores[(rank + 3) % n], T.cores[(rank - 3) % n]
    n_in = len(topo.engines(prv, core))
    n_out = len(topo.engines(core, nxt))
    rid, pid = topo.addr(nxt)[:2]
    queue = {"v": g.vector, "s": g.scalar, "p": g.tensor, "g": g, "y": g.sync}
    own_sem = {"v": "qv", "s": "qs", "p": "qp", "g": "qg"}
    total, seen, hist = {}, {}, {}

    def waits(q, me, reads, writes):
        need = {}
        for kind, recs in (("r", reads), ("w", writes)):
            for r in recs:
                bank = r[0] in PS
                for hk, hr, (sem, cnt), hq in hist.get(r[0], ()):
                    same = hq == me
                    if bank and not same:
                        pass
                    elif hk == "r" and kind == "r":
                        continue
                    elif same and (hk == "r" or (bank and q == "p")):
                        continue
                    elif not meets(hr, r):
                        continue
                    need[sem] = max(need.get(sem, 0), cnt)
        for sem, cnt in need.items():
            if seen.get((q, sem), 0) < cnt:
                queue[q].wait_ge(T.sem[sem], cnt)
                seen[(q, sem)] = cnt

    def note(me, tok, reads, writes):
        for kind, recs in (("r", reads), ("w", writes)):
            for r in recs:
                h = hist.setdefault(r[0], [])
                if r[0] in PS:
                    h = [e for e in h if e[3] == me]
                if kind == "w":
                    h = [e for e in h if not inside(e[1], r)]
                else:
                    h = [e for e in h if not (e[0] == "r" and e[3] == me and inside(e[1], r))]
                h.append((kind, r, tok, me))
                hist[r[0]] = h

    def emit(q, fn, reads, writes):
        waits(q, q, reads, writes)
        sem = own_sem[q]
        fn(queue[q]).then_inc(T.sem[sem], 1)
        total[sem] = total.get(sem, 0) + 1
        note(q, (sem, total[sem]), reads, writes)

    def load(q, sem, out, in_, reads, writes):
        waits(q, "dma" + sem, reads, writes)
        queue[q].dma_start(out, in_).then_inc(T.sem[sem], 16)
        total[sem] = 16
        note("dma" + sem, (sem, 16), reads, writes)

    def B(name, lo=0, hi=None, st=1):
        if name in COL:
            name, lo = COL[name]
            hi = lo + 1
        hi = (512 if name in PS else SB[name][0]) if hi is None else hi
        ap = T[name][:, lo:hi] if st == 1 else T[name][:, lo:hi:st]
        return ap, [(name, lo, hi, st)]

    def IND(win, off):
        return win[0].indirect(off[0]), win[1] + off[1]

    def wr(out):
        return out[1][:1]

    def copy(out, in_):
        emit("v", lambda e: e.tensor_copy(out[0], in_[0]), in_[1] + out[1][1:], wr(out))

    def tt(out, a, b, op):
        emit("v", lambda e: e.tensor_tensor(out[0], a[0], b[0], op), a[1] + b[1] + out[1][1:], wr(out))

    def ts(out, a, s1, s2, op0, op1=None):
        rd = list(a[1])
        if isinstance(s1, tuple):
            rd += s1[1]
            s1 = s1[0]
        if op1 is None:
            emit("v", lambda e: e.tensor_scalar(out[0], a[0], s1, None, op0), rd, wr(out))
        else:
            emit("v", lambda e: e.tensor_scalar(out[0], a[0], s1, s2, op0, op1), rd, wr(out))

    def scan(out, a, b, op0, op1, first=0.0):
        emit("v", lambda e: e.tensor_tensor_scan(out[0], a[0], b[0], first, op0, op1), a[1] + b[1], wr(out))

    def fill(out, c):
        emit("v", lambda e: e.memset(out[0], c), [], wr(out))

    def act(out, in_, func, bias=0.0, scale=1.0):
        rd = list(in_[1])
        if isinstance(scale, tuple):
            rd += scale[1]
            scale = scale[0]
        emit("s", lambda e: e.activation(out[0], in_[0], func, bias=bias, scale=scale), rd, wr(out))

    def mm(out, pairs):
        rd = []
        for a, b in pairs:
            rd += a[1] + b[1]

        def go(e):
            last = None
            for k, (a, b) in enumerate(pairs):
                last = e.matmul(out[0], a[0], b[0], k == 0, k == len(pairs) - 1)
            return last
        emit("p", go, rd, wr(out))

    def iota(out, pattern, base=0, cm=0):
        if SB[out[1][0][0]][1] == "int32":
            emit("g", lambda e: e.iota(out[0], pattern, base, cm), [], wr(out))
        else:
            emit("g", lambda e: e.iota(out[0], pattern, base, cm, allow_small_or_imprecise_dtypes=True), [], wr(out))

    def send(out_name, in_op, sem):
        waits("g", "rem", in_op[1], [])
        r = in_op[1][0]
        g.remote_dma(T[out_name][:, r[1]:r[2]], in_op[0], T.sem[sem], T.sem.sent, pid, rid, topo.mask(core, nxt))
        total["sent"] = total.get("sent", 0) + n_out

    def recv(name, lo, hi, sem):
        total[sem] = n_in
        note("rem", (sem, n_in), [], [(name, lo, hi, 1)])

    load("s", "ld_pf", T.pfb[:, 0:512], T.pf[:, 0:512], [], B("pfb")[1])
    load("y", "ld_pn", T.pnb[:, 0:512], T.pn[:, 0:512], [], B("pnb")[1])
    load("y", "ld_nb", T.nbi[:, 0:32], T.nb[:, 0:32], [], B("nbi")[1])
    load("s", "ld_fs", T.fsi[:, 0:32], T.fs[:, 0:32], [], B("fsi")[1])
    load("y", "ld_cb", T.cbi[:, 0:1024], T.cb[:, 0:1024], [], B("cbi")[1])
    load("y", "ld_bs", T.bsi[:, 0:64], T.bs[:, 0:64], [], B("bsi")[1])
    load("y", "ld_th", T.thi[:, 0:1], T.th[:, 0:1], [], B("thi")[1])
    for k in range(4):
        load("ys"[k % 2], "ld_x%d" % k, T.Xw[:, 2048 * k:2048 * k + 2048], T.xf[:, 2048 * k:2048 * k + 2048],
             [], B("Xw", 2048 * k, 2048 * k + 2048)[1])

    iota(B("pI"), [[0, 1]], 0, 1)
    iota(B("D0", 0, 2 * EL, 2), [[0, 2048]])
    iota(B("TM"), [[0, 4], [1, 32]])
    iota(B("gi"), [[0, 32], [1, 8]])
    iota(B("iot"), [[1, 1024]])
    iota(B("jb"), [[0, 32], [1, 16]])
    iota(B("mdiv"), [[1, 8], [0, 16]])
    iota(B("bji"), [[32, 4], [1, 16]])
    iota(B("qji"), [[1, 4]])
    iota(B("D0", 2 * EL, 4 * EL, 2), [[0, 2048]])
    iota(B("slotl"), [[256, 4], [16, 8]], 128)
    iota(B("n256"), [[256, 32]])
    for k in range(2, 4):
        iota(B("D0", 2 * EL * k, 2 * EL * (k + 1), 2), [[0, 2048]])
    iota(B("FJ"), [[0, 4096]])
    iota(B("LJ"), [[0, 4096]])
    iota(B("iotk"), [[2048, 1024]])
    iota(B("slot1"), [[256, 4], [1, 128]], 129)
    iota(B("Dri"), [[1, 16], [16, 128]])

    tt(B("c1"), B("pfb"), B("pnb"), OP.min)
    tt(B("c2"), B("pfb"), B("pnb"), OP.max)
    for k in range(11):
        act(B("D1", 2 * k + 1, 8 * EL, 32), B("c1"), AF.Copy)
    for k in range(16):
        copy(B("D0", 2 * k + 1, 8 * EL, 32), B("c2"))
    for k in range(11, 16):
        copy(B("D1", 2 * k + 1, 8 * EL, 32), B("c1"))
    copy(B("nu"), B("nbi"))
    for m in range(4):
        copy(B("AHi0", 256 * m, 256 * m + 128), IND(B("cbi"), B("nu", 8 * m, 8 * m + 8)))
    for m in range(4):
        copy(B("hu", 128 * m, 128 * m + 128), B("AHi0", 256 * m, 256 * m + 128))
    tt(B("swp"), B("pfb"), B("pnb"), OP.is_le)
    ts(B("sg"), B("swp"), 2.0, -1.0, OP.mult, OP.add)
    ts(B("pmI"), B("pI"), 15, None, OP.bitwise_and)
    ts(B("pqI"), B("pI"), 4, None, OP.logical_shift_right)
    copy(B("colm"), B("pmI"))
    copy(B("colq"), B("pqI"))

    def lane_constants():
        ts(B("E8"), B("gi", 0, 8), B("colq"), None, OP.is_equal)
        ts(B("E8n"), B("E8"), -1.0, None, OP.mult)
        for a in range(8):
            ts(B("SEn", a, 4096, 8), B("sg"), B("E8n", a, a + 1), None, OP.mult)
        ts(B("th2"), B("thi"), 2.0, 1.0, OP.mult, OP.add)
        ts(B("TM"), B("TM"), B("colm"), None, OP.is_equal)
        ts(B("thA"), B("th2"), 7, None, OP.arith_shift_right)
        ts(B("thB"), B("th2"), 127, None, OP.bitwise_and)
        ts(B("GE"), B("gi"), B("colq"), None, OP.is_equal)
        ts(B("thC"), B("thA"), -32.0, None, OP.mult)
        ts(B("thD"), B("thB"), -0.25, None, OP.mult)
        ts(B("THh"), B("TM"), B("thC"), None, OP.mult)
        ts(B("THl"), B("TM"), B("thD"), None, OP.mult)

    def flyer_constants():
        copy(B("bu"), B("bsi"))
        copy(B("fu"), B("fsi"))
        act(B("bigA"), IND(B("iot"), B("bu")), AF.Copy)
        ts(B("M16"), B("jb"), B("colm"), None, OP.is_equal)
        ts(B("R16"), B("jb"), 0.5, None, OP.is_gt)
        tt(B("tmp"), IND(B("bigA"), B("fu")), B("M16"), OP.mult)
        scan(B("tmp2"), B("R16"), B("tmp"), OP.mult, OP.add)
        copy(B("LSi0", 96, 128), B("tmp2", 15, 512, 16))
        copy(B("au"), B("LSi0", 96, 128))
        copy(B("A2f"), IND(B("cbi"), B("au")))
        copy(B("ao"), B("A2f"))

    def fold_constants():
        copy(B("colp"), B("pI"))
        ts(B("phI"), B("pI"), 5, None, OP.logical_shift_right)
        copy(B("colh"), B("phI"))
        ts(B("BJ"), B("bji"), B("colp"), None, OP.is_equal)
        ts(B("QJ"), B("qji"), B("colh"), None, OP.is_equal)
        for a in range(8):
            act(B("SEp", a, 4096, 8), B("sg"), AF.Copy, scale=B("E8", a, a + 1))

    def fold_blocks():
        for j in range(4):
            for a in range(8):
                lo = 128 * (8 * j + a) + 16 * a
                act(B("FJ", lo, lo + 16), B("BJ", 16 * j, 16 * j + 16), AF.Copy)
                lo = 128 * (4 * a + j) + 16 * a + 4 * j
                act(B("LJ", lo, lo + 4), B("QJ"), AF.Copy)

    def list_constants():
        fill(B("W"), 0.0)
        for k in range(16):
            copy(B("W", 129 * k, 128 * k + 128, 16), B("E8"))
        ts(B("BOb"), B("mdiv"), B("colq"), None, OP.is_equal)
        ts(B("Ib"), B("iot", 0, 128), B("colp"), None, OP.is_equal)
        ts(B("BOf"), B("mdiv"), B("colq"), None, OP.is_equal)
        copy(B("LSi0", 64, 96), B("fsi"))
        copy(B("LSi0", 32, 64), B("nbi"))
        copy(IND(B("bigB"), B("bu")), B("iot"))
        tt(B("tmp"), IND(B("bigB"), B("nu")), B("M16"), OP.mult)
        scan(B("tmp2"), B("R16"), B("tmp"), OP.mult, OP.add)
        copy(B("LSi0", 0, 32), B("tmp2", 15, 512, 16))
        ts(B("colm16"), B("colm"), 16.0, None, OP.mult)
        ts(B("baseI"), B("n256"), B("colm16"), None, OP.add)
        ts(B("own1"), B("slotl"), B("colm"), 1.0, OP.add, OP.add)
        mm(B("psM", 0, 32), [(B("W", 128 * r, 128 * r + 128), B("pfb", r, 512, 16)) for r in range(16)])
        copy(B("eI"), B("psM", 0, 32))
        ts(B("eJ"), B("eI"), 15, None, OP.bitwise_and)
        ts(B("eL2"), B("eJ"), 2.0, 16.0, OP.mult, OP.add)
        fill(B("E10"), 0.5)
        fill(B("r10"), 0.0)
        scan(B("p2i"), B("E10"), B("r10"), OP.mult, OP.add, 1.0)
        fill(B("fl", 0, 16), 2.0)
        scan(B("b1", 0, 16), B("fl", 0, 16), B("r10"), OP.mult, OP.add, 0.5)
        copy(B("pwI"), B("b1", 0, 16))

    def prep(t):
        L = "LSi%d" % t
        if t:
            copy(B("fu"), B(L, 64, 96))
            copy(B("au"), B(L, 96, 128))
        if t == 2:
            copy(B("cu"), B(L, 32, 64))
            copy(B("gu"), B(L, 0, 32))
            ts(B("cold"), B("colp"), 16.0, None, OP.mult)
            tt(B("cold"), B("cold"), B("colm"), OP.add)
            ts(B("Dri"), B("Dri"), B("cold"), None, OP.is_equal)
        copy(B("Fi"), B(L, 64, 96))
        for b in range(10):
            ts(B("VB", 32 * b, 32 * b + 32), B("Fi"), b, 1, OP.arith_shift_right, OP.bitwise_and)
        ts(B("U"), B("VB"), -2.0, 1.0, OP.mult, OP.add)
        tt(B("F0"), B(L, 64, 96), B("U", 0, 32), OP.add)
        tt(B("DQP"), B(L, 0, 64), B(L, 64, 128), OP.subtract)
        tt(B("val"), IND(B("iotk"), B("au")), B("slot1"), OP.add)
        if t == 2:
            act(B("jb"), IND(B("iot"), B("cu")), AF.Copy)
            copy(IND(B("bigB"), B("gu")), B("jb"))

    def gather(e):
        c = e % NCH
        off = B("hu" if e < NCH else "ao", 64 * c, 64 * c + 64)
        act(B("D1", EL * c, EL * c + EL, 2), IND(B("Xw"), off), AF.Copy)

    def cast_h(t, m):
        recv("AHi%d" % t, 256 * m, 256 * m + 256, "ah%d_%d" % (t, m))
        copy(B("hu", 128 * m, 128 * m + 128), B("AHi%d" % t, 256 * m, 256 * m + 128))

    zn = [0]

    def clamp(c):
        z = "Z%d" % (zn[0] % NZ)
        zn[0] += 1
        scan(B(z), B("D0", EL * c, EL * c + EL), B("D1", EL * c, EL * c + EL), OP.min, OP.max)
        return z

    def lanes(e, z):
        c = e % NCH
        bank = "psR%d" % (c // 2)
        se = "SEn" if e < NCH else "SEp"

        def go(p):
            last = None
            if e < NCH and c % 2 == 0:
                p.matmul(T[bank][:, 0:256], T.THh[:, 0:128], T.GE[:, 0:256], True, False)
            for k in range(64):
                i = 64 * (c % 2) + k
                q, j = i // 4, i % 4
                last = p.matmul(T[bank][32 * j:32 * j + 16, 8 * q:8 * q + 8], T[z][:, 32 * k + 1:32 * k + 32:2],
                                T[se][:, 512 * c + 8 * k:512 * c + 8 * k + 8], False, False)
            if e >= NCH and c % 2:
                last = p.matmul(T[bank][:, 0:256], T.THl[:, 0:128], T.GE[:, 0:256], False, True)
            return last
        emit("p", go, [(z, 0, EL, 1), (se, 512 * c, 512 * c + 512, 1)] + B("THh")[1] + B("THl")[1] + B("GE")[1], [(bank, 0, 256, 1)])

    def h_col(u, flyer):
        lo = 256 * u + 128 * flyer
        return lo, lo + 128

    def swaps(u):
        act(B("swR", 256 * u, 256 * u + 256), B("psR%d" % u, 0, 256), AF.Sign)

    def fold(h):
        def go(p):
            last = None
            for j in range(4):
                for a in range(8):
                    lo = 128 * (8 * j + a)
                    last = p.matmul(T["psC%d" % h][:, j:256:4], T.FJ[:, lo:lo + 128], T.swR[:, 512 * h + a:512 * h + 512:8], a == 0, a == 7)
            return last
        emit("p", go, B("FJ")[1] + B("swR", 512 * h, 512 * h + 512)[1], [("psC%d" % h, 0, 256, 1)])

    def natural(h):
        act(B("swp", 256 * h, 256 * h + 256), B("psC%d" % h, 0, 256), AF.Copy)

    def sums(h):
        mm(B("psC%d" % h, 256, 512), [(B("BOb"), B("swp", 256 * h, 256 * h + 256))])

    def signs(t, h):
        b = "psC%d" % h
        if t < 2:
            act(B(b, 0, 256), B(b, 256, 512), AF.Sign, bias=5.0)
        act(B("sgf", 256 * h, 256 * h + 256), B(b, 256, 512), AF.Sign, bias=1.0)

    def diff(t, u):
        lo, hi = 128 * u, 128 * u + 128
        tt(B("dHA", lo, hi), B("AHi%d" % t, *h_col(u, 0)), B("A2f", lo, hi), OP.subtract)

    def post(t, u):
        b = "psC%d" % (u // 2)
        x, y = 128 * (u % 2), 256 + 128 * (u % 2)
        lo, hi = 128 * u, 128 * u + 128
        if t < 2:
            tt(B(b, y, y + 128), B("swp", lo, hi), B(b, x, x + 128), OP.is_equal)
        else:
            ts(B(b, y, y + 128), B("swp", lo, hi), 0.0, None, OP.is_gt)
        tt(B(b, x, x + 128), B("dHA", lo, hi), B(b, y, y + 128), OP.mult)
        out = "AHo%d" % t
        tt(B(out, *h_col(u, 0)), B("AHi%d" % t, *h_col(u, 0)), B(b, x, x + 128), OP.subtract)
        tt(B(out, *h_col(u, 1)), B("A2f", lo, hi), B(b, x, x + 128), OP.add)
        if t < 2:
            send("AHi%d" % (t + 1), B(out, 256 * u, 256 * u + 256), "ah%d_%d" % (t + 1, u))
        else:
            copy(IND(B("bigA"), B("cu", 8 * u, 8 * u + 8)), B(out, 256 * u, 256 * u + 128))
            copy(IND(B("bigA"), B("au", 8 * u, 8 * u + 8)), B(out, 256 * u + 128, 256 * u + 256))

    def lists(n0, n1):
        mm(B("psL", n0, n1), [(B("W", 128 * r, 128 * r + 128), B("swp", 16 * n0 + r, 16 * n1, 16)) for r in range(16)])

    def lists_direct(n0, n1):
        def go(p):
            last = None
            for a in range(8):
                for j in range(4):
                    lo = 128 * (4 * a + j)
                    last = p.matmul(T.psL[:, n0:n1], T.LJ[:, lo:lo + 128], T.swR[:, 32 * n0 + 8 * j + a:32 * n1:32], a + j == 0, a + j == 10)
            return last
        emit("p", go, B("LJ")[1] + B("swR", 32 * n0, 32 * n1)[1], [("psL", n0, n1, 1)])

    def frames(n0, n1):
        tt(B("o1", n0, n1), B("eL2", n0, n1), B("psL", n0, n1), OP.add)
        ts(B("o2", n0, n1), B("o1", n0, n1), 1, 15, OP.arith_shift_right, OP.bitwise_and)
        tt(B("o3", n0, n1), B("o2", n0, n1), B("baseI", n0, n1), OP.add)
        copy(B("offU", n0, n1), B("o3", n0, n1))

    def put_frames(n0, n1):
        copy(IND(B("Xw"), B("offU", n0, n1)), B("pfb", 16 * n0, 16 * n1))

    def mark(n0, n1):
        tt(IND(B("tab"), B("fu", n0, n1)), B("val", 16 * n0, 16 * n1), B("sgf", 16 * n0, 16 * n1), OP.mult)

    def partner_a(t):
        L, O = "LSi%d" % t, "LSo%d" % t
        psl = B("psL", 0, 32)
        emit("v", lambda e: e.tensor_reduce(B("red")[0], psl[0], AxisListType.X, OP.add), psl[1], B("red")[1])
        ts(B("r10", 1, 10), B("p2i", 1, 10), B("red"), None, OP.mult)
        mm(B("psM", 1, 10), [(B("BOf"), B("r10", 1, 10))])
        ts(B("T2", 0, 32), B("psL", 0, 32), -5.0, None, OP.is_lt)
        ts(B("T2", 32, 64), B("psL", 0, 32), -5.0, None, OP.is_lt)
        ts(B("fl"), B("psL", 0, 32), -1.0, None, OP.is_gt)
        ts(B("yI", 1, 10), B("psM", 1, 10), -0.5 + 2.0 ** -11, None, OP.add)
        tt(B("td"), B("T2"), B("DQP"), OP.mult)
        ts(B("bI", 1, 10), B("yI", 1, 10), 1, None, OP.bitwise_and)
        copy(B(O, 128, 160), B("own1"))
        tt(B("E10", 1, 10), B("bI", 1, 10), B("pwI", 1, 10), OP.mult)
        for k in range(1, 10):
            act(B("XB", 32 * k, 32 * k + 32), B("U", 32 * k, 32 * k + 32), AF.Copy, scale=B("E10", k, k + 1))
        mm(B("psM", 32, 64), [(B("Ib"), B("XB", 32 * k, 32 * k + 32)) for k in range(1, 10)])
        tt(B(O, 64, 128), B(L, 64, 128), B("td"), OP.add)
        tt(B(O, 0, 64), B(L, 0, 64), B("td"), OP.subtract)
        if t == 2:
            load("y", "st_yf", T.yf[:, 0:32], T.LSo2[:, 64:96], B(O, 64, 96)[1], [])
            load("y", "st_yn", T.yn[:, 0:32], T.LSo2[:, 32:64], B(O, 32, 64)[1], [])

    def partner_b(t):
        L, O = "LSi%d" % t, "LSo%d" % t
        tt(B("Xl"), B("F0"), B("psM", 32, 64), OP.add)
        copy(B("Xu"), B("Xl"))
        tt(B("tmp"), IND(B("tab"), B("Xu")), B("M16"), OP.mult)
        scan(B("tmp2"), B("R16"), B("tmp"), OP.mult, OP.add)
        q = B("tmp2", 15, 512, 16)
        ts(B("b1"), q, 0.5, None, OP.is_gt)
        copy(B("qi"), q)
        tt(B("BB", 0, 32), B("b1"), B("fl"), OP.mult)
        ts(B("dec", 0, 32), B("qi"), 11, None, OP.arith_shift_right)
        if t < 2:
            tt(B("BB", 32, 64), B("b1"), B("fl"), OP.mult)
            ts(B("dec", 32, 64), B("qi"), 2047, None, OP.bitwise_and)
            tt(B("df"), B("dec"), B(O, 96, 160), OP.subtract)
            tt(B("df2"), B("df"), B("BB"), OP.mult)
            tt(B(O, 96, 160), B(O, 96, 160), B("df2"), OP.add)
            send("LSi%d" % (t + 1), B(O, 0, 160), "ls%d" % (t + 1))
            return
        tt(B("df", 0, 32), B("dec", 0, 32), B(L, 96, 128), OP.subtract)
        tt(B("df2", 0, 32), B("df", 0, 32), B("BB", 0, 32), OP.mult)
        tt(B("asf"), B(L, 96, 128), B("df2", 0, 32), OP.add)
        copy(B("asu"), B("asf"))
        copy(B("tmp"), IND(B("iot"), B("asu")))
        copy(IND(B("bigB"), B("fu")), B("tmp"))
        mm(B("psM", 64, 128), [(B("Dri", 128 * r, 128 * r + 128), B("bigB", r, 1024, 16)) for r in range(16)])
        copy(B("ybo"), B("psM", 64, 128))
        load("y", "st_yb", T.yb[:, 0:64], T.ybo[:, 0:64], B("ybo")[1], [])

    for t in range(3):
        if t == 0:
            iota(B("tab"), [[0, 1024]])
            for e in range(LOOK):
                gather(e)
        for e in range(2 * NCH):
            c = e % NCH
            z = clamp(c)
            if e < NCH:
                if t == 0 and e == 0:
                    lane_constants()
                if t == 0 and e == 2:
                    flyer_constants()
                if t == 0 and e == 3:
                    fold_constants()
                lanes(e, z)
                if t == 0 and e == 5:
                    list_constants()
                if t == 0 and e == 6:
                    fold_blocks()
                if t and e == 0:
                    partner_b(t - 1)
                    iota(B("tab"), [[0, 1024]])
                if t and e == 1:
                    cast_h(t, 2)
                if t and e == 3:
                    cast_h(t, 3)
                if t and e == 4:
                    recv("LSi%d" % t, 0, 160, "ls%d" % t)
                    ts(B("pu"), B("LSi%d" % t, 128, 160), -1.0, None, OP.add)
                    copy(B("ao"), IND(B("AHi%d" % t), B("pu")))
                gather(e + LOOK)
                if t and e == 5:
                    act(B("A2f"), IND(B("AHi%d" % t), B("pu")), AF.Copy)
                continue
            u = c // 2
            if c == 4:
                prep(t)
                fold(0)
            if c == 5:
                sums(0)
            lanes(e, z)
            if e + LOOK < 2 * NCH:
                gather(e + LOOK)
            if c == 5:
                signs(t, 0)
            if c % 2:
                swaps(u)
            if c < 4:
                diff(t, c)
            if c == 4:
                natural(0)
            if c == 5:
                lists(0, 16)
            if c == 7 and t < 2:
                frames(0, 16)
            if c >= 6:
                post(t, c - 6)
        lists_direct(16, 32)
        fold(1)
        natural(1)
        sums(1)
        signs(t, 1)
        if t < 2:
            put_frames(0, 16)
            mark(0, 16)
            frames(16, 32)
            put_frames(16, 32)
            cast_h(t + 1, 0)
            gather(0)
            partner_a(t)
            cast_h(t + 1, 1)
            for e in range(1, LOOK):
                gather(e)
            post(t, 2)
            post(t, 3)
            mark(16, 32)
        else:
            mark(0, 16)
            partner_a(t)
            mark(16, 32)
            partner_b(t)
            post(t, 2)
            post(t, 3)
            load("y", "st_yc", T.yc[:, 0:1024], T.bigA[:, 0:1024], B("bigA")[1], [])
    for sem, cnt in total.items():
        g.wait_ge(T.sem[sem], cnt)
